import numpy as np
import ml_dtypes


def mxq(x, axis, fmt="e4m3"):
    dtype, down = {"e4m3": (ml_dtypes.float8_e4m3fn, 7), "e5m2": (ml_dtypes.float8_e5m2, 14)}[fmt]
    v = np.moveaxis(np.asarray(x, np.float32).astype(ml_dtypes.bfloat16).astype(np.float64), axis, -1)
    blocks = v.reshape(v.shape[:-1] + (-1, 32))
    amax = np.abs(blocks).max(-1, keepdims=True)
    byte = np.maximum(np.where(amax > 0, np.frexp(amax)[1] - 1 + 127, 0) - down, 1)
    scale = np.exp2(byte - 127.0)
    codes = (blocks / scale).astype(np.float32).astype(dtype).astype(np.float64)
    return np.moveaxis((codes * scale).reshape(v.shape), -1, axis)


WIDE = False


def mx_kscale(k):
    if not WIDE:
        return np.ones(k)
    levels = np.array([10, -10, 5, -5, 0])
    if k % 512:
        return np.exp2(np.random.permutation(np.resize(levels, k // 32))).repeat(32)
    a = np.empty((k // 512, 16))
    for p in range(k // 512):
        a[p, :8] = np.random.permutation(np.resize(levels, 8))
        for g in range(8):
            far = levels[np.abs(levels - a[p, g]) >= 10]
            a[p, g + 8] = far[np.random.randint(len(far))]
    return np.exp2(a.ravel()).repeat(32)


def f64(x):
    return np.asarray(x).astype(np.float64)


def striped(idx):
    return np.tile(idx.reshape(-1, 16).T, (8, 1)).astype(np.uint16)


def unstriped(offs):
    return offs[:16].T.reshape(-1).astype(np.int64)


def pack_weight(w):
    k, n = w.shape
    w = f64(np.asarray(w, np.float32).astype(ml_dtypes.bfloat16)).reshape(k // 32, 32, n)
    amax = np.abs(w).max(1)
    byte = np.clip(np.where(amax > 0, np.frexp(amax)[1] - 1 + 127 - 7, 1), 1, 254)
    scaled = (w * np.exp2(127.0 - byte)[:, None, :]).reshape(k, n).astype(np.float32)
    words = np.ascontiguousarray(scaled.reshape(k // 512, 128, 4, n).transpose(0, 1, 3, 2)).astype(ml_dtypes.float8_e4m3fn).view(np.uint8)
    return words, np.ascontiguousarray(byte.astype(np.uint8).reshape(k // 512, 16, n))


def unpack_weight(words, scales):
    g, p, n, _ = words.shape
    vals = np.ascontiguousarray(words).view(ml_dtypes.float8_e4m3fn).astype(np.float64) * np.repeat(np.exp2(scales.astype(np.float64) - 127.0), 8, axis=1)[..., None]
    return vals.transpose(0, 1, 3, 2).reshape(g * 512, n)


def relu(v):
    return np.maximum(v, 0.0)


K, T, S, D, N, H, V, U = 512, 2048, 1024, 4, 256, 512, 256, 512


def setup_inputs():
    n = np.random.standard_normal
    s = mx_kscale(K)[:, None]
    u = mx_kscale(H)
    packed_xT = pack_weight(n((K, T)) * s)
    return {
        "x_words": packed_xT[0],
        "x_scales": packed_xT[1],
        "w1": (n((K, H)) / np.sqrt(K) / s).astype(np.float32),
        "cap": (np.random.uniform(0.6, 1.4, (H, S))).astype(np.float32),
        "fr": (np.random.uniform(0.5, 2.0, (H, U))).astype(np.float32),
        "unit": (np.random.uniform(0.6, 1.4, (H, 1)) * u[:, None]).astype(np.float32),
        "w2": (n((H, N)) / np.sqrt(H) / u[:, None]).astype(np.float32),
        "offs": striped(np.random.permutation(T)[:S]),
        "aln": striped(np.random.permutation(S)),
        "rep_": striped(np.random.permutation(np.concatenate([np.arange(V), np.random.randint(0, V, U - V)]))),
    }


def reference(x_words, x_scales, w1, cap, fr, unit, w2, offs, aln, rep_):
    xq = unpack_weight(x_words, x_scales)[:, unstriped(offs)]
    y = mxq(f64(w1), 0, "e4m3").T @ xq
    ya = y[:, unstriped(aln)]
    sub = np.minimum(np.abs(y - ya), f64(cap))
    gap = relu(ya)
    cost = sub + 0.4 * gap
    dist = cost.reshape(len(cost), -1, D).sum(axis=2)
    kern = np.exp(-0.6 * dist)
    kr = kern[:, unstriped(rep_)]
    hid = f64(unit) * (kr * f64(fr))
    return mxq(f64(w2), 0, "e4m3").T @ mxq(hid, 0, "e4m3")

@@ -1,0 +1,251 @@
+from contextlib import ExitStack
+
+import concourse.mybir as mybir
+from concourse.masks import make_identity
+
+K, T, S, D, N, H, V, U = 512, 2048, 1024, 4, 256, 512, 256, 512
+FLOPS = 2 * K * H * S + 2 * H * N * U
+
+F32 = mybir.dt.float32
+BF16 = mybir.dt.bfloat16
+I32 = mybir.dt.int32
+U32 = mybir.dt.uint32
+U16 = mybir.dt.uint16
+U8 = mybir.dt.uint8
+FP8X4 = mybir.dt.float8_e4m3fn_x4
+ALU = mybir.AluOpType
+ACT = mybir.ActivationFunctionType
+
+P = 128
+PACK = 4
+HALF = S // 2
+GROUPS = HALF // D
+CLONES = U // 2
+SPARE = 16
+
+
+def tile_picked_ycdrcp_rad_p_kernel(
+    tc, x_words, x_scales, w1, cap, fr, unit, w2, offs, aln, rep_, out
+):
+    nc = tc.nc
+    with ExitStack() as ctx:
+        lists = ctx.enter_context(tc.tile_pool(name="lists", bufs=1))
+        keep = ctx.enter_context(tc.tile_pool(name="keep", bufs=1))
+        ring = ctx.enter_context(tc.tile_pool(name="ring", bufs=3))
+        psum = ctx.enter_context(tc.psum_pool(name="psum", bufs=1))
+
+        offs_t = lists.tile([P, S // 16], U16, name="offs_t")
+        aln_t = lists.tile([P, S // 16], U16, name="aln_t")
+        rep_t = lists.tile([P, U // 16], U16, name="rep_t")
+
+        table_scales = keep.tile([P, T], U8, name="table_scales", align_bytes=64)
+        nc.gpsimd.memset(table_scales[:].bitcast(I32), 0)
+        nc.sync.dma_start(offs_t[:], offs)
+        for q in range(4):
+            nc.sync.dma_start(
+                table_scales[32 * q : 32 * q + 4, :].bitcast(I32),
+                x_scales[0, 4 * q : 4 * q + 4, :].bitcast(I32),
+            )
+        table_words = keep.tile([P, T], I32, name="table_words", align_bytes=64)
+        nc.sync.dma_start(table_words[:], x_words[0].rearrange("p n t -> p (n t)").bitcast(I32))
+        w1_raw = keep.tile([P, PACK, H], F32, name="w1_raw")
+        nc.sync.dma_start(w1_raw[:], w1.rearrange("(p j) c -> p j c", j=PACK))
+        nc.sync.dma_start(aln_t[:], aln)
+        cap_rows = cap.rearrange("(p t) s -> p t s", t=PACK)
+        cap_t = []
+        for t in range(PACK):
+            tile = keep.tile([P, S], F32, name="cap%d" % t)
+            nc.sync.dma_start(tile[:], cap_rows[:, t, :])
+            cap_t.append(tile)
+        nc.sync.dma_start(rep_t[:], rep_)
+        unit_t = keep.tile([P, PACK], F32, name="unit_t")
+        nc.sync.dma_start(unit_t[:], unit.rearrange("(p t) o -> p (t o)", t=PACK))
+        fr_t = keep.tile([P, PACK, U], F32, name="fr_t")
+        nc.sync.dma_start(fr_t[:], fr.rearrange("(p t) r -> p t r", t=PACK))
+        w2_raw = keep.tile([P, PACK, N], F32, name="w2_raw")
+        nc.sync.dma_start(w2_raw[:], w2.rearrange("(p j) c -> p j c", j=PACK))
+
+        ident = keep.tile([P, P], F32, name="ident")
+        make_identity(nc, ident[:])
+        kern = []
+        for t in range(PACK):
+            tile = keep.tile([P, V + SPARE], F32, name="kern%d" % t)
+            nc.gpsimd.memset(tile[:, V:], 0.0)
+            kern.append(tile)
+
+        picked_scales = keep.tile([P, S], U8, name="picked_scales", align_bytes=64)
+        nc.vector.tensor_copy(picked_scales[:], table_scales[:].indirect(offs_t[:]))
+        picked_words = []
+        for h in range(2):
+            tile = keep.tile([P, HALF], U32, name="picked_words%d" % h, align_bytes=64)
+            nc.vector.tensor_copy(
+                tile[:], table_words[:].bitcast(U32).indirect(offs_t[:, h * HALF // 16 : (h + 1) * HALF // 16])
+            )
+            picked_words.append(tile)
+
+        w1_src = w1_raw[:].rearrange("p j (m t) -> p m j t", t=PACK)
+        w1_codes, w1_scales, w1_bf = [], [], []
+        for a in range(2):
+            tile = keep.tile([P, 2, P, PACK], BF16, name="w1_bf%d" % a, align_bytes=64)
+            dst = tile[:].rearrange("p t m j -> p m j t")
+            src = w1_src[:, :, :, 2 * a : 2 * a + 2]
+            if a == 0:
+                nc.vector.tensor_copy(dst, src)
+            else:
+                nc.scalar.copy(dst, src)
+            w1_bf.append(tile)
+
+        def quantise_w1(a):
+            codes = keep.tile([P, 2 * P], U32, name="w1_codes%d" % a, align_bytes=64)
+            scales = keep.tile([P, 2 * P], U8, name="w1_scales%d" % a, align_bytes=64)
+            nc.vector.quantize_mx(
+                out=codes[:].bitcast(FP8X4), scales=scales[:], in_=w1_bf[a][:].rearrange("p t m j -> p (t m j)")
+            )
+            w1_codes.append(codes)
+            w1_scales.append(scales)
+
+        y_bank, y_sb, ya, diff, mag, sub, gap, kern_T = {}, {}, {}, {}, {}, {}, {}, {}
+        dist_bank, kern_bank = {}, {}
+        hid = [keep.tile([P, PACK, CLONES], F32, name="hid%d" % h) for h in range(2)]
+
+        def product(t):
+            cols = slice((t % 2) * P, (t % 2 + 1) * P)
+            y_sb[t] = keep.tile([P, S], F32, name="y%d" % t)
+            for h in range(2):
+                bank = psum.tile([P, HALF], F32, name="y_bank", tag="bank%d%d" % (t % 2, h))
+                nc.tensor.matmul_mx(
+                    out=bank[:],
+                    lhsT=w1_codes[t // 2][:, cols].bitcast(FP8X4),
+                    lhsT_scale=w1_scales[t // 2][:, cols],
+                    rhs=picked_words[h][:].bitcast(FP8X4),
+                    rhs_scale=picked_scales[:, h * HALF : (h + 1) * HALF],
+                    start=True,
+                    stop=True,
+                )
+                y_bank[t, h] = bank
+                dst = y_sb[t][:, h * HALF : (h + 1) * HALF]
+                if t == 0 and h == 1:
+                    nc.vector.tensor_copy(dst, bank[:])
+                else:
+                    nc.scalar.copy(dst, bank[:])
+
+        def align(t, h):
+            ya[t, h] = keep.tile([P, HALF], F32, name="ya%d%d" % (t, h))
+            src = y_sb[t][:].indirect(aln_t[:, h * HALF // 16 : (h + 1) * HALF // 16])
+            if t == 0 and h == 1:
+                nc.vector.tensor_copy(ya[t, h][:], src)
+            else:
+                nc.scalar.activation(ya[t, h][:], src, ACT.Copy)
+
+        def difference(t, h):
+            diff[t, h] = ring.tile([P, HALF], F32, name="diff")
+            nc.vector.tensor_tensor(diff[t, h][:], ya[t, h][:], y_bank[t, h][:], ALU.subtract)
+            gap[t, h] = ring.tile([P, D, GROUPS], F32, name="gap")
+            nc.vector.tensor_scalar(
+                gap[t, h][:].rearrange("p d v -> p v d"),
+                ya[t, h][:].rearrange("p (v d) -> p v d", d=D),
+                0.0,
+                0.4,
+                ALU.max,
+                ALU.mult,
+            )
+
+        def magnitude(t, h):
+            mag[t, h] = ring.tile([P, HALF], F32, name="mag")
+            nc.scalar.activation(mag[t, h][:], diff[t, h][:], ACT.Abs)
+
+        def distance(t, h):
+            sub[t, h] = ring.tile([P, D, GROUPS], F32, name="sub")
+            nc.vector.tensor_tensor(
+                sub[t, h][:].rearrange("p d v -> p v d"),
+                mag[t, h][:].rearrange("p (v d) -> p v d", d=D),
+                cap_t[t][:, h * HALF : (h + 1) * HALF].rearrange("p (v d) -> p v d", d=D),
+                ALU.min,
+            )
+            dist_bank[t, h] = psum.tile([P, P], F32, name="dist_bank", tag="dist%d" % h)
+            terms = [gap[t, h][:, d, :] for d in range(D)] + [sub[t, h][:, d, :] for d in range(D)]
+            for n, term in enumerate(terms):
+                nc.tensor.matmul(
+                    dist_bank[t, h][:], lhsT=term, rhs=ident[:], start=(n == 0), stop=(n == len(terms) - 1), is_transpose=True
+                )
+
+        def kernel_value(t, h):
+            kern_T[t, h] = ring.tile([P, P], F32, name="kern_T")
+            nc.scalar.activation(kern_T[t, h][:], dist_bank[t, h][:], ACT.Exp, scale=-0.6)
+            if h == 0:
+                kern_bank[t] = psum.tile([P, V], F32, name="kern_bank", tag="kern")
+            nc.tensor.transpose(kern_bank[t][:, h * GROUPS : (h + 1) * GROUPS], kern_T[t, h][:], ident[:])
+
+        def clones(t):
+            nc.vector.tensor_scalar(kern[t][:, :V], kern_bank[t][:], unit_t[:, t : t + 1], None, ALU.mult)
+            for h in range(2):
+                nc.vector.tensor_tensor(
+                    hid[h][:, t, :],
+                    kern[t][:].indirect(rep_t[:, h * CLONES // 16 : (h + 1) * CLONES // 16]),
+                    fr_t[:, t, h * CLONES : (h + 1) * CLONES],
+                    ALU.mult,
+                )
+
+        quantise_w1(0)
+        product(0)
+        quantise_w1(1)
+        steps = [(t, h) for t in range(PACK) for h in range(2)]
+        for n in range(len(steps) + 4):
+            if n < len(steps):
+                t, h = steps[n]
+                align(t, h)
+                if h == 1 and t + 1 < PACK:
+                    product(t + 1)
+            if 0 <= n - 1 < len(steps):
+                difference(*steps[n - 1])
+                magnitude(*steps[n - 1])
+            if 0 <= n - 2 < len(steps):
+                distance(*steps[n - 2])
+            if 0 <= n - 3 < len(steps):
+                t, h = steps[n - 3]
+                kernel_value(t, h)
+            if 0 <= n - 4 < len(steps):
+                t, h = steps[n - 4]
+                if h == 1:
+                    clones(t)
+            if n == 6:
+                w2_bf = keep.tile([P, N, PACK], BF16, name="w2_bf", align_bytes=64)
+                nc.vector.tensor_copy(
+                    w2_bf[:].rearrange("p (c i) j -> p c j i", i=4), w2_raw[:].rearrange("p j (c i) -> p c j i", i=4)
+                )
+            if n == 7:
+                w2_codes = keep.tile([P, N], U32, name="w2_codes", align_bytes=64)
+                w2_scales = keep.tile([P, N], U8, name="w2_scales", align_bytes=64)
+                nc.vector.quantize_mx(
+                    out=w2_codes[:].bitcast(FP8X4), scales=w2_scales[:], in_=w2_bf[:].rearrange("p c j -> p (c j)")
+                )
+
+        hid_bf = []
+        for h in range(2):
+            tile = keep.tile([P, CLONES, PACK], BF16, name="hid_bf%d" % h, align_bytes=64)
+            nc.vector.tensor_copy(
+                tile[:].rearrange("p (c i) t -> p c t i", i=4), hid[h][:].rearrange("p t (c i) -> p c t i", i=4)
+            )
+            hid_bf.append(tile)
+        for h in range(2):
+            codes = keep.tile([P, CLONES], U32, name="hid_codes%d" % h, align_bytes=64)
+            scales = keep.tile([P, CLONES], U8, name="hid_scales%d" % h, align_bytes=64)
+            nc.vector.quantize_mx(out=codes[:].bitcast(FP8X4), scales=scales[:], in_=hid_bf[h][:].rearrange("p c t -> p (c t)"))
+            for b in range(N // P):
+                rows = slice(b * P, (b + 1) * P)
+                bank = psum.tile([P, CLONES], F32, name="out_bank", tag="bank%d%d" % (b, h))
+                nc.tensor.matmul_mx(
+                    out=bank[:],
+                    lhsT=w2_codes[:, rows].bitcast(FP8X4),
+                    lhsT_scale=w2_scales[:, rows],
+                    rhs=codes[:].bitcast(FP8X4),
+                    rhs_scale=scales[:],
+                    start=True,
+                    stop=True,
+                )
+                result = keep.tile([P, CLONES], F32, name="result%d%d" % (b, h))
+                if h == 1 and b == 1:
+                    nc.vector.tensor_copy(result[:], bank[:])
+                else:
+                    nc.scalar.copy(result[:], bank[:])
+                nc.sync.dma_start(out[rows, h * CLONES : (h + 1) * CLONES], result[:])

@@ -22,6 +22,11 @@ HALF = S // 2
 GROUPS = HALF // D
 CLONES = U // 2
 SPARE = 16
+PIECES = ((0, 512), (512, 768), (768, 1024))
+
+
+def entries(offsets, first, last):
+    return offsets[:, first // 16 : last // 16]
 
 
 def tile_picked_ycdrcp_rad_p_kernel(
@@ -31,7 +36,6 @@ def tile_picked_ycdrcp_rad_p_kernel(
     with ExitStack() as ctx:
         lists = ctx.enter_context(tc.tile_pool(name="lists", bufs=1))
         keep = ctx.enter_context(tc.tile_pool(name="keep", bufs=1))
-        ring = ctx.enter_context(tc.tile_pool(name="ring", bufs=3))
         psum = ctx.enter_context(tc.psum_pool(name="psum", bufs=1))
 
         offs_t = lists.tile([P, S // 16], U16, name="offs_t")
@@ -41,29 +45,29 @@ def tile_picked_ycdrcp_rad_p_kernel(
         table_scales = keep.tile([P, T], U8, name="table_scales", align_bytes=64)
         nc.gpsimd.memset(table_scales[:].bitcast(I32), 0)
         nc.sync.dma_start(offs_t[:], offs)
+        table_words = keep.tile([P, T], I32, name="table_words", align_bytes=64)
+        nc.sync.dma_start(table_words[:], x_words[0].rearrange("p n t -> p (n t)").bitcast(I32))
+        nc.sync.dma_start(aln_t[:], aln)
+        nc.sync.dma_start(rep_t[:], rep_)
         for q in range(4):
             nc.sync.dma_start(
                 table_scales[32 * q : 32 * q + 4, :].bitcast(I32),
                 x_scales[0, 4 * q : 4 * q + 4, :].bitcast(I32),
             )
-        table_words = keep.tile([P, T], I32, name="table_words", align_bytes=64)
-        nc.sync.dma_start(table_words[:], x_words[0].rearrange("p n t -> p (n t)").bitcast(I32))
         w1_raw = keep.tile([P, PACK, H], F32, name="w1_raw")
         nc.sync.dma_start(w1_raw[:], w1.rearrange("(p j) c -> p j c", j=PACK))
-        nc.sync.dma_start(aln_t[:], aln)
+        w2_raw = keep.tile([P, PACK, N], F32, name="w2_raw")
+        nc.sync.dma_start(w2_raw[:], w2.rearrange("(p j) c -> p j c", j=PACK))
         cap_rows = cap.rearrange("(p t) s -> p t s", t=PACK)
         cap_t = []
         for t in range(PACK):
             tile = keep.tile([P, S], F32, name="cap%d" % t)
             nc.sync.dma_start(tile[:], cap_rows[:, t, :])
             cap_t.append(tile)
-        nc.sync.dma_start(rep_t[:], rep_)
         unit_t = keep.tile([P, PACK], F32, name="unit_t")
         nc.sync.dma_start(unit_t[:], unit.rearrange("(p t) o -> p (t o)", t=PACK))
         fr_t = keep.tile([P, PACK, U], F32, name="fr_t")
         nc.sync.dma_start(fr_t[:], fr.rearrange("(p t) r -> p t r", t=PACK))
-        w2_raw = keep.tile([P, PACK, N], F32, name="w2_raw")
-        nc.sync.dma_start(w2_raw[:], w2.rearrange("(p j) c -> p j c", j=PACK))
 
         ident = keep.tile([P, P], F32, name="ident")
         make_identity(nc, ident[:])
@@ -73,26 +77,14 @@ def tile_picked_ycdrcp_rad_p_kernel(
             nc.gpsimd.memset(tile[:, V:], 0.0)
             kern.append(tile)
 
-        picked_scales = keep.tile([P, S], U8, name="picked_scales", align_bytes=64)
-        nc.vector.tensor_copy(picked_scales[:], table_scales[:].indirect(offs_t[:]))
-        picked_words = []
-        for h in range(2):
-            tile = keep.tile([P, HALF], U32, name="picked_words%d" % h, align_bytes=64)
-            nc.vector.tensor_copy(
-                tile[:], table_words[:].bitcast(U32).indirect(offs_t[:, h * HALF // 16 : (h + 1) * HALF // 16])
-            )
-            picked_words.append(tile)
+        picked_words = keep.tile([P, S], U32, name="picked_words", align_bytes=64)
+        nc.vector.tensor_copy(picked_words[:], table_words[:].bitcast(U32).indirect(offs_t[:]))
 
         w1_src = w1_raw[:].rearrange("p j (m t) -> p m j t", t=PACK)
         w1_codes, w1_scales, w1_bf = [], [], []
         for a in range(2):
             tile = keep.tile([P, 2, P, PACK], BF16, name="w1_bf%d" % a, align_bytes=64)
-            dst = tile[:].rearrange("p t m j -> p m j t")
-            src = w1_src[:, :, :, 2 * a : 2 * a + 2]
-            if a == 0:
-                nc.vector.tensor_copy(dst, src)
-            else:
-                nc.scalar.copy(dst, src)
+            nc.scalar.copy(tile[:].rearrange("p t m j -> p m j t"), w1_src[:, :, :, 2 * a : 2 * a + 2])
             w1_bf.append(tile)
 
         def quantise_w1(a):
@@ -104,126 +96,131 @@ def tile_picked_ycdrcp_rad_p_kernel(
             w1_codes.append(codes)
             w1_scales.append(scales)
 
-        y_bank, y_sb, ya, diff, mag, sub, gap, kern_T = {}, {}, {}, {}, {}, {}, {}, {}
+        picked_scales = []
+        for n, (first, last) in enumerate(PIECES):
+            if n == len(PIECES) - 1:
+                quantise_w1(0)
+            tile = keep.tile([P, last - first], U8, name="picked_scales%d" % n, align_bytes=64, tag="w1_bf0" if n == len(PIECES) - 1 else "picked_scales%d" % n)
+            nc.vector.tensor_copy(tile[:], table_scales[:].indirect(entries(offs_t, first, last)))
+            picked_scales.append(tile)
+
+        y_sb, ya, diff, mag, sub, gap, kern_T = {}, {}, {}, {}, {}, {}, {}
         dist_bank, kern_bank = {}, {}
-        hid = [keep.tile([P, PACK, CLONES], F32, name="hid%d" % h) for h in range(2)]
 
         def product(t):
             cols = slice((t % 2) * P, (t % 2 + 1) * P)
             y_sb[t] = keep.tile([P, S], F32, name="y%d" % t)
-            for h in range(2):
-                bank = psum.tile([P, HALF], F32, name="y_bank", tag="bank%d%d" % (t % 2, h))
+            for n, (first, last) in enumerate(PIECES):
+                if n < 2 or t == 0:
+                    bank = psum.tile([P, HALF], F32, name="y_bank", tag="y%d" % ((0, 1, 2), (1, 2), (1, 2), (1, 2))[t][n])
+                    base = first
                 nc.tensor.matmul_mx(
-                    out=bank[:],
+                    out=bank[:, first - base : last - base],
                     lhsT=w1_codes[t // 2][:, cols].bitcast(FP8X4),
                     lhsT_scale=w1_scales[t // 2][:, cols],
-                    rhs=picked_words[h][:].bitcast(FP8X4),
-                    rhs_scale=picked_scales[:, h * HALF : (h + 1) * HALF],
+                    rhs=picked_words[:, first:last].bitcast(FP8X4),
+                    rhs_scale=picked_scales[n][:],
                     start=True,
                     stop=True,
                 )
-                y_bank[t, h] = bank
-                dst = y_sb[t][:, h * HALF : (h + 1) * HALF]
-                if t == 0 and h == 1:
-                    nc.vector.tensor_copy(dst, bank[:])
-                else:
-                    nc.scalar.copy(dst, bank[:])
+                if t == 0 and n == 0:
+                    nc.vector.tensor_copy(y_sb[t][:, base:last], bank[:, : last - base])
+                elif n != 1 or t == 0:
+                    nc.scalar.copy(y_sb[t][:, base:last], bank[:, : last - base])
 
         def align(t, h):
             ya[t, h] = keep.tile([P, HALF], F32, name="ya%d%d" % (t, h))
-            src = y_sb[t][:].indirect(aln_t[:, h * HALF // 16 : (h + 1) * HALF // 16])
-            if t == 0 and h == 1:
+            src = y_sb[t][:].indirect(entries(aln_t, h * HALF, (h + 1) * HALF))
+            if h == 1:
                 nc.vector.tensor_copy(ya[t, h][:], src)
             else:
                 nc.scalar.activation(ya[t, h][:], src, ACT.Copy)
 
         def difference(t, h):
-            diff[t, h] = ring.tile([P, HALF], F32, name="diff")
-            nc.vector.tensor_tensor(diff[t, h][:], ya[t, h][:], y_bank[t, h][:], ALU.subtract)
-            gap[t, h] = ring.tile([P, D, GROUPS], F32, name="gap")
-            nc.vector.tensor_scalar(
-                gap[t, h][:].rearrange("p d v -> p v d"),
-                ya[t, h][:].rearrange("p (v d) -> p v d", d=D),
-                0.0,
-                0.4,
-                ALU.max,
-                ALU.mult,
-            )
+            diff[t, h] = keep.tile([P, HALF], F32, align_bytes=64, name="diff%d%d" % (t, h))
+            nc.vector.tensor_tensor(diff[t, h][:], ya[t, h][:], y_sb[t][:, h * HALF : (h + 1) * HALF], ALU.subtract)
+
+        def gap_cost(t, h):
+            gap[t, h] = keep.tile([P, 2, GROUPS, 2], F32, name="gap%d%d" % (t, h))
+            dst = gap[t, h][:].rearrange("p a v b -> p v a b")
+            src = ya[t, h][:].rearrange("p (v a b) -> p v a b", a=2, b=2)
+            if False:
+                nc.scalar.activation(dst, src, ACT.Relu, scale=0.4)
+            else:
+                nc.vector.tensor_scalar(dst, src, 0.0, 0.4, ALU.max, ALU.mult)
 
         def magnitude(t, h):
-            mag[t, h] = ring.tile([P, HALF], F32, name="mag")
+            mag[t, h] = keep.tile([P, HALF], F32, align_bytes=64, name="mag%d%d" % (t, h))
             nc.scalar.activation(mag[t, h][:], diff[t, h][:], ACT.Abs)
 
         def distance(t, h):
-            sub[t, h] = ring.tile([P, D, GROUPS], F32, name="sub")
+            sub[t, h] = keep.tile([P, 2, GROUPS, 2], F32, name="sub%d%d" % (t, h))
             nc.vector.tensor_tensor(
-                sub[t, h][:].rearrange("p d v -> p v d"),
-                mag[t, h][:].rearrange("p (v d) -> p v d", d=D),
-                cap_t[t][:, h * HALF : (h + 1) * HALF].rearrange("p (v d) -> p v d", d=D),
+                sub[t, h][:].rearrange("p a v b -> p v a b"),
+                mag[t, h][:].rearrange("p (v a b) -> p v a b", a=2, b=2),
+                cap_t[t][:, h * HALF : (h + 1) * HALF].rearrange("p (v a b) -> p v a b", a=2, b=2),
                 ALU.min,
             )
-            dist_bank[t, h] = psum.tile([P, P], F32, name="dist_bank", tag="dist%d" % h)
-            terms = [gap[t, h][:, d, :] for d in range(D)] + [sub[t, h][:, d, :] for d in range(D)]
+            dist_bank[t, h] = psum.tile([P, P], F32, name="dist_bank", tag="dist%d%d" % (t % 2, h))
+            terms = [tile[:, a, :, b] for tile in (gap[t, h], sub[t, h]) for a in range(2) for b in range(2)]
             for n, term in enumerate(terms):
                 nc.tensor.matmul(
                     dist_bank[t, h][:], lhsT=term, rhs=ident[:], start=(n == 0), stop=(n == len(terms) - 1), is_transpose=True
                 )
 
         def kernel_value(t, h):
-            kern_T[t, h] = ring.tile([P, P], F32, name="kern_T")
+            kern_T[t, h] = keep.tile([P, P], F32, name="kern_T%d%d" % (t, h))
             nc.scalar.activation(kern_T[t, h][:], dist_bank[t, h][:], ACT.Exp, scale=-0.6)
             if h == 0:
                 kern_bank[t] = psum.tile([P, V], F32, name="kern_bank", tag="kern")
             nc.tensor.transpose(kern_bank[t][:, h * GROUPS : (h + 1) * GROUPS], kern_T[t, h][:], ident[:])
 
-        def clones(t):
-            nc.vector.tensor_scalar(kern[t][:, :V], kern_bank[t][:], unit_t[:, t : t + 1], None, ALU.mult)
-            for h in range(2):
-                nc.vector.tensor_tensor(
-                    hid[h][:, t, :],
-                    kern[t][:].indirect(rep_t[:, h * CLONES // 16 : (h + 1) * CLONES // 16]),
-                    fr_t[:, t, h * CLONES : (h + 1) * CLONES],
-                    ALU.mult,
-                )
+        def scale_rows(t):
+            nc.scalar.activation(kern[t][:, :V], kern_bank[t][:], ACT.Copy, scale=unit_t[:, t : t + 1])
 
-        quantise_w1(0)
         product(0)
         quantise_w1(1)
-        steps = [(t, h) for t in range(PACK) for h in range(2)]
-        for n in range(len(steps) + 4):
-            if n < len(steps):
-                t, h = steps[n]
-                align(t, h)
-                if h == 1 and t + 1 < PACK:
-                    product(t + 1)
-            if 0 <= n - 1 < len(steps):
-                difference(*steps[n - 1])
-                magnitude(*steps[n - 1])
-            if 0 <= n - 2 < len(steps):
-                distance(*steps[n - 2])
-            if 0 <= n - 3 < len(steps):
-                t, h = steps[n - 3]
-                kernel_value(t, h)
-            if 0 <= n - 4 < len(steps):
-                t, h = steps[n - 4]
+        w2_bf = keep.tile([P, N, PACK], BF16, name="w2_bf", align_bytes=64)
+        nc.scalar.copy(
+            w2_bf[:].rearrange("p (c i) j -> p c j i", i=4), w2_raw[:].rearrange("p j (c i) -> p c j i", i=4)
+        )
+        w2_codes = keep.tile([P, N], U32, name="w2_codes", align_bytes=64)
+        w2_scales = keep.tile([P, N], U8, name="w2_scales", align_bytes=64)
+        nc.vector.quantize_mx(
+            out=w2_codes[:].bitcast(FP8X4), scales=w2_scales[:], in_=w2_bf[:].rearrange("p c j -> p (c j)")
+        )
+        for t in range(PACK + 1):
+            if t < PACK:
+                align(t, 0)
+                align(t, 1)
+            if t >= 1:
+                distance(t - 1, 0)
+                distance(t - 1, 1)
+            if t + 1 < PACK:
+                product(t + 1)
+            if t < PACK:
+                for step in (difference, gap_cost, magnitude):
+                    step(t, 0)
+                    step(t, 1)
+            if t >= 1:
+                kernel_value(t - 1, 0)
+                kernel_value(t - 1, 1)
+                scale_rows(t - 1)
+
+        hid = [keep.tile([P, PACK, CLONES], F32, name="hid%d" % h) for h in range(2)]
+        for t in range(PACK):
+            for h in range(2):
+                src = kern[t][:].indirect(entries(rep_t, h * CLONES, (h + 1) * CLONES))
                 if h == 1:
-                    clones(t)
-            if n == 6:
-                w2_bf = keep.tile([P, N, PACK], BF16, name="w2_bf", align_bytes=64)
-                nc.vector.tensor_copy(
-                    w2_bf[:].rearrange("p (c i) j -> p c j i", i=4), w2_raw[:].rearrange("p j (c i) -> p c j i", i=4)
-                )
-            if n == 7:
-                w2_codes = keep.tile([P, N], U32, name="w2_codes", align_bytes=64)
-                w2_scales = keep.tile([P, N], U8, name="w2_scales", align_bytes=64)
-                nc.vector.quantize_mx(
-                    out=w2_codes[:].bitcast(FP8X4), scales=w2_scales[:], in_=w2_bf[:].rearrange("p c j -> p (c j)")
-                )
+                    looked_up = keep.tile([P, CLONES], F32, align_bytes=64, name="looked_up%d%d" % (t, h), tag=("diff31", "diff30", "mag31", "lu3")[t])
+                    nc.scalar.activation(looked_up[:], src, ACT.Copy)
+                    src = looked_up[:]
+                nc.vector.tensor_tensor(hid[h][:, t, :], src, fr_t[:, t, h * CLONES : (h + 1) * CLONES], ALU.mult)
 
         hid_bf = []
         for h in range(2):
             tile = keep.tile([P, CLONES, PACK], BF16, name="hid_bf%d" % h, align_bytes=64)
-            nc.vector.tensor_copy(
+            (nc.scalar.copy if h == 0 else nc.vector.tensor_copy)(
                 tile[:].rearrange("p (c i) t -> p c t i", i=4), hid[h][:].rearrange("p t (c i) -> p c t i", i=4)
             )
             hid_bf.append(tile)
@@ -233,7 +230,7 @@ def tile_picked_ycdrcp_rad_p_kernel(
             nc.vector.quantize_mx(out=codes[:].bitcast(FP8X4), scales=scales[:], in_=hid_bf[h][:].rearrange("p c t -> p (c t)"))
             for b in range(N // P):
                 rows = slice(b * P, (b + 1) * P)
-                bank = psum.tile([P, CLONES], F32, name="out_bank", tag="bank%d%d" % (b, h))
+                bank = psum.tile([P, CLONES], F32, name="out_bank", tag=("y0", "y1", "y2", "dist00")[2 * h + b])
                 nc.tensor.matmul_mx(
                     out=bank[:],
                     lhsT=w2_codes[:, rows].bitcast(FP8X4),
@@ -244,7 +241,7 @@ def tile_picked_ycdrcp_rad_p_kernel(
                     stop=True,
                 )
                 result = keep.tile([P, CLONES], F32, name="result%d%d" % (b, h))
-                if h == 1 and b == 1:
+                if b == 1:
                     nc.vector.tensor_copy(result[:], bank[:])
                 else:
                     nc.scalar.copy(result[:], bank[:])

@@ -22,6 +22,7 @@ HALF = S // 2
 GROUPS = HALF // D
 CLONES = U // 2
 SPARE = 16
+QUARTER = U // 4
 PIECES = ((0, 512), (512, 768), (768, 1024))
 
 
@@ -54,26 +55,26 @@ def tile_picked_ycdrcp_rad_p_kernel(
                 table_scales[32 * q : 32 * q + 4, :].bitcast(I32),
                 x_scales[0, 4 * q : 4 * q + 4, :].bitcast(I32),
             )
-        w1_raw = keep.tile([P, PACK, H], F32, name="w1_raw")
+        w1_raw = keep.tile([P, PACK, H], F32, align_bytes=64, name="w1_raw")
         nc.sync.dma_start(w1_raw[:], w1.rearrange("(p j) c -> p j c", j=PACK))
-        w2_raw = keep.tile([P, PACK, N], F32, name="w2_raw")
+        w2_raw = keep.tile([P, PACK, N], F32, align_bytes=64, name="w2_raw")
         nc.sync.dma_start(w2_raw[:], w2.rearrange("(p j) c -> p j c", j=PACK))
         cap_rows = cap.rearrange("(p t) s -> p t s", t=PACK)
         cap_t = []
         for t in range(PACK):
-            tile = keep.tile([P, S], F32, name="cap%d" % t)
+            tile = keep.tile([P, S], F32, align_bytes=64, name="cap%d" % t)
             nc.sync.dma_start(tile[:], cap_rows[:, t, :])
             cap_t.append(tile)
-        unit_t = keep.tile([P, PACK], F32, name="unit_t")
+        unit_t = keep.tile([P, PACK], F32, align_bytes=64, name="unit_t")
         nc.sync.dma_start(unit_t[:], unit.rearrange("(p t) o -> p (t o)", t=PACK))
-        fr_t = keep.tile([P, PACK, U], F32, name="fr_t")
+        fr_t = keep.tile([P, PACK, U], F32, align_bytes=64, name="fr_t")
         nc.sync.dma_start(fr_t[:], fr.rearrange("(p t) r -> p t r", t=PACK))
 
-        ident = keep.tile([P, P], F32, name="ident")
+        ident = keep.tile([P, P], F32, align_bytes=64, name="ident")
         make_identity(nc, ident[:])
         kern = []
         for t in range(PACK):
-            tile = keep.tile([P, V + SPARE], F32, name="kern%d" % t)
+            tile = keep.tile([P, V + SPARE], F32, align_bytes=64, name="kern%d" % t)
             nc.gpsimd.memset(tile[:, V:], 0.0)
             kern.append(tile)
 
@@ -109,7 +110,7 @@ def tile_picked_ycdrcp_rad_p_kernel(
 
         def product(t):
             cols = slice((t % 2) * P, (t % 2 + 1) * P)
-            y_sb[t] = keep.tile([P, S], F32, name="y%d" % t)
+            y_sb[t] = keep.tile([P, S], F32, align_bytes=64, name="y%d" % t)
             for n, (first, last) in enumerate(PIECES):
                 if n < 2 or t == 0:
                     bank = psum.tile([P, HALF], F32, name="y_bank", tag="y%d" % ((0, 1, 2), (1, 2), (1, 2), (1, 2))[t][n])
@@ -129,22 +130,26 @@ def tile_picked_ycdrcp_rad_p_kernel(
                     nc.scalar.copy(y_sb[t][:, base:last], bank[:, : last - base])
 
         def align(t, h):
-            ya[t, h] = keep.tile([P, HALF], F32, name="ya%d%d" % (t, h))
-            src = y_sb[t][:].indirect(entries(aln_t, h * HALF, (h + 1) * HALF))
-            if h == 1:
-                nc.vector.tensor_copy(ya[t, h][:], src)
-            else:
-                nc.scalar.activation(ya[t, h][:], src, ACT.Copy)
+            if h == 0:
+                ya[t] = keep.tile([P, S], F32, align_bytes=64, name="ya%d" % t)
+            split = (512, 640, 640, 512)[t]
+            pieces = [(0, split)] if h == 0 else [(split, S)]
+            for first, last in pieces:
+                src = y_sb[t][:].indirect(entries(aln_t, first, last))
+                if h == 1:
+                    nc.vector.tensor_copy(ya[t][:, first:last], src)
+                else:
+                    nc.scalar.activation(ya[t][:, first:last], src, ACT.Copy)
 
         def difference(t, h):
             diff[t, h] = keep.tile([P, HALF], F32, align_bytes=64, name="diff%d%d" % (t, h))
-            nc.vector.tensor_tensor(diff[t, h][:], ya[t, h][:], y_sb[t][:, h * HALF : (h + 1) * HALF], ALU.subtract)
+            nc.vector.tensor_tensor(diff[t, h][:], ya[t][:, h * HALF : (h + 1) * HALF], y_sb[t][:, h * HALF : (h + 1) * HALF], ALU.subtract)
 
         def gap_cost(t, h):
-            gap[t, h] = keep.tile([P, 2, GROUPS, 2], F32, name="gap%d%d" % (t, h))
-            dst = gap[t, h][:].rearrange("p a v b -> p v a b")
-            src = ya[t, h][:].rearrange("p (v a b) -> p v a b", a=2, b=2)
-            if False:
+            gap[t, h] = keep.tile([P, D, GROUPS], F32, align_bytes=64, name="gap%d%d" % (t, h))
+            dst = gap[t, h][:].rearrange("p d v -> p v d")
+            src = ya[t][:, h * HALF : (h + 1) * HALF].rearrange("p (v d) -> p v d", d=D)
+            if t == 3 and h == 1:
                 nc.scalar.activation(dst, src, ACT.Relu, scale=0.4)
             else:
                 nc.vector.tensor_scalar(dst, src, 0.0, 0.4, ALU.max, ALU.mult)
@@ -154,7 +159,7 @@ def tile_picked_ycdrcp_rad_p_kernel(
             nc.scalar.activation(mag[t, h][:], diff[t, h][:], ACT.Abs)
 
         def distance(t, h):
-            sub[t, h] = keep.tile([P, 2, GROUPS, 2], F32, name="sub%d%d" % (t, h))
+            sub[t, h] = keep.tile([P, 2, GROUPS, 2], F32, align_bytes=64, name="sub%d%d" % (t, h))
             nc.vector.tensor_tensor(
                 sub[t, h][:].rearrange("p a v b -> p v a b"),
                 mag[t, h][:].rearrange("p (v a b) -> p v a b", a=2, b=2),
@@ -162,14 +167,14 @@ def tile_picked_ycdrcp_rad_p_kernel(
                 ALU.min,
             )
             dist_bank[t, h] = psum.tile([P, P], F32, name="dist_bank", tag="dist%d%d" % (t % 2, h))
-            terms = [tile[:, a, :, b] for tile in (gap[t, h], sub[t, h]) for a in range(2) for b in range(2)]
+            terms = [gap[t, h][:, d, :] for d in range(D)] + [sub[t, h][:, a, :, b] for a in range(2) for b in range(2)]
             for n, term in enumerate(terms):
                 nc.tensor.matmul(
                     dist_bank[t, h][:], lhsT=term, rhs=ident[:], start=(n == 0), stop=(n == len(terms) - 1), is_transpose=True
                 )
 
         def kernel_value(t, h):
-            kern_T[t, h] = keep.tile([P, P], F32, name="kern_T%d%d" % (t, h))
+            kern_T[t, h] = keep.tile([P, P], F32, align_bytes=64, name="kern_T%d%d" % (t, h))
             nc.scalar.activation(kern_T[t, h][:], dist_bank[t, h][:], ACT.Exp, scale=-0.6)
             if h == 0:
                 kern_bank[t] = psum.tile([P, V], F32, name="kern_bank", tag="kern")
@@ -207,32 +212,35 @@ def tile_picked_ycdrcp_rad_p_kernel(
                 kernel_value(t - 1, 1)
                 scale_rows(t - 1)
 
-        hid = [keep.tile([P, PACK, CLONES], F32, name="hid%d" % h) for h in range(2)]
+        hid = keep.tile([P, PACK, U], F32, align_bytes=64, name="hid", tag="diff30")
         for t in range(PACK):
-            for h in range(2):
-                src = kern[t][:].indirect(entries(rep_t, h * CLONES, (h + 1) * CLONES))
-                if h == 1:
-                    looked_up = keep.tile([P, CLONES], F32, align_bytes=64, name="looked_up%d%d" % (t, h), tag=("diff31", "diff30", "mag31", "lu3")[t])
+            width = CLONES if t < PACK - 1 else QUARTER
+            for first in range(0, U, width):
+                cols = slice(first, first + width)
+                src = kern[t][:].indirect(entries(rep_t, first, first + width))
+                if first >= CLONES and t != 2:
+                    looked_up = keep.tile([P, width], F32, align_bytes=64, name="looked_up", tag=(("diff31", "mag31", "lu2", "lu3")[t]) if t < 3 else "lu3%d" % first)
                     nc.scalar.activation(looked_up[:], src, ACT.Copy)
                     src = looked_up[:]
-                nc.vector.tensor_tensor(hid[h][:, t, :], src, fr_t[:, t, h * CLONES : (h + 1) * CLONES], ALU.mult)
+                nc.vector.tensor_tensor(hid[:, t, cols], src, fr_t[:, t, cols], ALU.mult)
 
-        hid_bf = []
-        for h in range(2):
-            tile = keep.tile([P, CLONES, PACK], BF16, name="hid_bf%d" % h, align_bytes=64)
-            (nc.scalar.copy if h == 0 else nc.vector.tensor_copy)(
-                tile[:].rearrange("p (c i) t -> p c t i", i=4), hid[h][:].rearrange("p t (c i) -> p c t i", i=4)
+        hid_bf = {}
+        for q in range(4):
+            hid_bf[q] = keep.tile([P, QUARTER, PACK], BF16, name="hid_bf%d" % q, align_bytes=64)
+            (nc.scalar.copy if q % 2 == 0 else nc.vector.tensor_copy)(
+                hid_bf[q][:].rearrange("p (c i) t -> p c t i", i=4),
+                hid[:, :, q * QUARTER : (q + 1) * QUARTER].rearrange("p t (c i) -> p c t i", i=4),
             )
-            hid_bf.append(tile)
-        for h in range(2):
-            codes = keep.tile([P, CLONES], U32, name="hid_codes%d" % h, align_bytes=64)
-            scales = keep.tile([P, CLONES], U8, name="hid_scales%d" % h, align_bytes=64)
-            nc.vector.quantize_mx(out=codes[:].bitcast(FP8X4), scales=scales[:], in_=hid_bf[h][:].rearrange("p c t -> p (c t)"))
+        out_rows = out.rearrange("(b p) r -> p b r", p=P)
+        for q in range(4):
+            codes = keep.tile([P, QUARTER], U32, name="hid_codes%d" % q, align_bytes=64)
+            scales = keep.tile([P, QUARTER], U8, name="hid_scales%d" % q, align_bytes=64)
+            nc.vector.quantize_mx(out=codes[:].bitcast(FP8X4), scales=scales[:], in_=hid_bf[q][:].rearrange("p c t -> p (c t)"))
+            bank = psum.tile([P, N // P, QUARTER], F32, name="out_bank", tag=("y0", "y1", "y2", "dist00")[q])
             for b in range(N // P):
                 rows = slice(b * P, (b + 1) * P)
-                bank = psum.tile([P, CLONES], F32, name="out_bank", tag=("y0", "y1", "y2", "dist00")[2 * h + b])
                 nc.tensor.matmul_mx(
-                    out=bank[:],
+                    out=bank[:, b, :],
                     lhsT=w2_codes[:, rows].bitcast(FP8X4),
                     lhsT_scale=w2_scales[:, rows],
                     rhs=codes[:].bitcast(FP8X4),
@@ -240,9 +248,9 @@ def tile_picked_ycdrcp_rad_p_kernel(
                     start=True,
                     stop=True,
                 )
-                result = keep.tile([P, CLONES], F32, name="result%d%d" % (b, h))
-                if b == 1:
-                    nc.vector.tensor_copy(result[:], bank[:])
-                else:
-                    nc.scalar.copy(result[:], bank[:])
-                nc.sync.dma_start(out[rows, h * CLONES : (h + 1) * CLONES], result[:])
+            result = keep.tile([P, N // P, QUARTER], F32, align_bytes=64, name="result%d" % q)
+            if q == 3:
+                nc.vector.tensor_copy(result[:], bank[:])
+            else:
+                nc.scalar.copy(result[:], bank[:])
+            nc.sync.dma_start(out_rows[:, :, q * QUARTER : (q + 1) * QUARTER], result[:])

from contextlib import ExitStack

import concourse.mybir as mybir
from concourse.masks import make_identity

K, T, S, D, N, H, V, U = 512, 2048, 1024, 4, 256, 512, 256, 512
FLOPS = 2 * K * H * S + 2 * H * N * U

F32 = mybir.dt.float32
BF16 = mybir.dt.bfloat16
I32 = mybir.dt.int32
U32 = mybir.dt.uint32
U16 = mybir.dt.uint16
U8 = mybir.dt.uint8
FP8X4 = mybir.dt.float8_e4m3fn_x4
ALU = mybir.AluOpType
ACT = mybir.ActivationFunctionType

P = 128
PACK = 4
HALF = S // 2
GROUPS = HALF // D
CLONES = U // 2
SPARE = 16
QUARTER = U // 4
PIECES = ((0, 512), (512, 768), (768, 1024))


def entries(offsets, first, last):
    return offsets[:, first // 16 : last // 16]


def tile_picked_ycdrcp_rad_p_kernel(
    tc, x_words, x_scales, w1, cap, fr, unit, w2, offs, aln, rep_, out
):
    nc = tc.nc
    with ExitStack() as ctx:
        lists = ctx.enter_context(tc.tile_pool(name="lists", bufs=1))
        keep = ctx.enter_context(tc.tile_pool(name="keep", bufs=1))
        psum = ctx.enter_context(tc.psum_pool(name="psum", bufs=1))

        offs_t = lists.tile([P, S // 16], U16, name="offs_t")
        aln_t = lists.tile([P, S // 16], U16, name="aln_t")
        rep_t = lists.tile([P, U // 16], U16, name="rep_t")

        table_scales = keep.tile([P, T], U8, name="table_scales", align_bytes=64)
        nc.gpsimd.memset(table_scales[:].bitcast(I32), 0)
        nc.sync.dma_start(offs_t[:], offs)
        table_words = keep.tile([P, T], I32, name="table_words", align_bytes=64)
        nc.sync.dma_start(table_words[:], x_words[0].rearrange("p n t -> p (n t)").bitcast(I32))
        nc.sync.dma_start(aln_t[:], aln)
        nc.sync.dma_start(rep_t[:], rep_)
        for q in range(4):
            nc.sync.dma_start(
                table_scales[32 * q : 32 * q + 4, :].bitcast(I32),
                x_scales[0, 4 * q : 4 * q + 4, :].bitcast(I32),
            )
        w1_raw = keep.tile([P, PACK, H], F32, align_bytes=64, name="w1_raw")
        nc.sync.dma_start(w1_raw[:], w1.rearrange("(p j) c -> p j c", j=PACK))
        w2_raw = keep.tile([P, PACK, N], F32, align_bytes=64, name="w2_raw")
        nc.sync.dma_start(w2_raw[:], w2.rearrange("(p j) c -> p j c", j=PACK))
        cap_rows = cap.rearrange("(p t) s -> p t s", t=PACK)
        cap_t = []
        for t in range(PACK):
            tile = keep.tile([P, S], F32, align_bytes=64, name="cap%d" % t)
            nc.sync.dma_start(tile[:], cap_rows[:, t, :])
            cap_t.append(tile)
        unit_t = keep.tile([P, PACK], F32, align_bytes=64, name="unit_t")
        nc.sync.dma_start(unit_t[:], unit.rearrange("(p t) o -> p (t o)", t=PACK))
        fr_t = keep.tile([P, PACK, U], F32, align_bytes=64, name="fr_t")
        nc.sync.dma_start(fr_t[:], fr.rearrange("(p t) r -> p t r", t=PACK))

        ident = keep.tile([P, P], F32, align_bytes=64, name="ident")
        make_identity(nc, ident[:])
        kern = []
        for t in range(PACK):
            tile = keep.tile([P, V + SPARE], F32, align_bytes=64, name="kern%d" % t)
            nc.gpsimd.memset(tile[:, V:], 0.0)
            kern.append(tile)

        picked_words = keep.tile([P, S], U32, name="picked_words", align_bytes=64)
        nc.vector.tensor_copy(picked_words[:], table_words[:].bitcast(U32).indirect(offs_t[:]))

        w1_src = w1_raw[:].rearrange("p j (m t) -> p m j t", t=PACK)
        w1_codes, w1_scales, w1_bf = [], [], []
        for a in range(2):
            tile = keep.tile([P, 2, P, PACK], BF16, name="w1_bf%d" % a, align_bytes=64)
            nc.scalar.copy(tile[:].rearrange("p t m j -> p m j t"), w1_src[:, :, :, 2 * a : 2 * a + 2])
            w1_bf.append(tile)

        def quantise_w1(a):
            codes = keep.tile([P, 2 * P], U32, name="w1_codes%d" % a, align_bytes=64)
            scales = keep.tile([P, 2 * P], U8, name="w1_scales%d" % a, align_bytes=64)
            nc.vector.quantize_mx(
                out=codes[:].bitcast(FP8X4), scales=scales[:], in_=w1_bf[a][:].rearrange("p t m j -> p (t m j)")
            )
            w1_codes.append(codes)
            w1_scales.append(scales)

        picked_scales = []
        for n, (first, last) in enumerate(PIECES):
            if n == len(PIECES) - 1:
                quantise_w1(0)
            tile = keep.tile([P, last - first], U8, name="picked_scales%d" % n, align_bytes=64, tag="w1_bf0" if n == len(PIECES) - 1 else "picked_scales%d" % n)
            nc.vector.tensor_copy(tile[:], table_scales[:].indirect(entries(offs_t, first, last)))
            picked_scales.append(tile)

        y_sb, ya, diff, mag, sub, gap, kern_T = {}, {}, {}, {}, {}, {}, {}
        dist_bank, kern_bank = {}, {}

        def product(t):
            cols = slice((t % 2) * P, (t % 2 + 1) * P)
            y_sb[t] = keep.tile([P, S], F32, align_bytes=64, name="y%d" % t)
            for n, (first, last) in enumerate(PIECES):
                if n < 2 or t == 0:
                    bank = psum.tile([P, HALF], F32, name="y_bank", tag="y%d" % ((0, 1, 2), (1, 2), (1, 2), (1, 2))[t][n])
                    base = first
                nc.tensor.matmul_mx(
                    out=bank[:, first - base : last - base],
                    lhsT=w1_codes[t // 2][:, cols].bitcast(FP8X4),
                    lhsT_scale=w1_scales[t // 2][:, cols],
                    rhs=picked_words[:, first:last].bitcast(FP8X4),
                    rhs_scale=picked_scales[n][:],
                    start=True,
                    stop=True,
                )
                if t == 0 and n == 0:
                    nc.vector.tensor_copy(y_sb[t][:, base:last], bank[:, : last - base])
                elif n != 1 or t == 0:
                    nc.scalar.copy(y_sb[t][:, base:last], bank[:, : last - base])

        def align(t, h):
            if h == 0:
                ya[t] = keep.tile([P, S], F32, align_bytes=64, name="ya%d" % t)
            split = (512, 640, 640, 512)[t]
            pieces = [(0, split)] if h == 0 else [(split, S)]
            for first, last in pieces:
                src = y_sb[t][:].indirect(entries(aln_t, first, last))
                if h == 1:
                    nc.vector.tensor_copy(ya[t][:, first:last], src)
                else:
                    nc.scalar.activation(ya[t][:, first:last], src, ACT.Copy)

        def difference(t, h):
            diff[t, h] = keep.tile([P, HALF], F32, align_bytes=64, name="diff%d%d" % (t, h))
            nc.vector.tensor_tensor(diff[t, h][:], ya[t][:, h * HALF : (h + 1) * HALF], y_sb[t][:, h * HALF : (h + 1) * HALF], ALU.subtract)

        def gap_cost(t, h):
            gap[t, h] = keep.tile([P, D, GROUPS], F32, align_bytes=64, name="gap%d%d" % (t, h))
            dst = gap[t, h][:].rearrange("p d v -> p v d")
            src = ya[t][:, h * HALF : (h + 1) * HALF].rearrange("p (v d) -> p v d", d=D)
            if t == 3 and h == 1:
                nc.scalar.activation(dst, src, ACT.Relu, scale=0.4)
            else:
                nc.vector.tensor_scalar(dst, src, 0.0, 0.4, ALU.max, ALU.mult)

        def magnitude(t, h):
            mag[t, h] = keep.tile([P, HALF], F32, align_bytes=64, name="mag%d%d" % (t, h))
            nc.scalar.activation(mag[t, h][:], diff[t, h][:], ACT.Abs)

        def distance(t, h):
            sub[t, h] = keep.tile([P, 2, GROUPS, 2], F32, align_bytes=64, name="sub%d%d" % (t, h))
            nc.vector.tensor_tensor(
                sub[t, h][:].rearrange("p a v b -> p v a b"),
                mag[t, h][:].rearrange("p (v a b) -> p v a b", a=2, b=2),
                cap_t[t][:, h * HALF : (h + 1) * HALF].rearrange("p (v a b) -> p v a b", a=2, b=2),
                ALU.min,
            )
            dist_bank[t, h] = psum.tile([P, P], F32, name="dist_bank", tag="dist%d%d" % (t % 2, h))
            terms = [gap[t, h][:, d, :] for d in range(D)] + [sub[t, h][:, a, :, b] for a in range(2) for b in range(2)]
            for n, term in enumerate(terms):
                nc.tensor.matmul(
                    dist_bank[t, h][:], lhsT=term, rhs=ident[:], start=(n == 0), stop=(n == len(terms) - 1), is_transpose=True
                )

        def kernel_value(t, h):
            kern_T[t, h] = keep.tile([P, P], F32, align_bytes=64, name="kern_T%d%d" % (t, h))
            nc.scalar.activation(kern_T[t, h][:], dist_bank[t, h][:], ACT.Exp, scale=-0.6)
            if h == 0:
                kern_bank[t] = psum.tile([P, V], F32, name="kern_bank", tag="kern")
            nc.tensor.transpose(kern_bank[t][:, h * GROUPS : (h + 1) * GROUPS], kern_T[t, h][:], ident[:])

        def scale_rows(t):
            nc.scalar.activation(kern[t][:, :V], kern_bank[t][:], ACT.Copy, scale=unit_t[:, t : t + 1])

        product(0)
        quantise_w1(1)
        w2_bf = keep.tile([P, N, PACK], BF16, name="w2_bf", align_bytes=64)
        nc.scalar.copy(
            w2_bf[:].rearrange("p (c i) j -> p c j i", i=4), w2_raw[:].rearrange("p j (c i) -> p c j i", i=4)
        )
        w2_codes = keep.tile([P, N], U32, name="w2_codes", align_bytes=64)
        w2_scales = keep.tile([P, N], U8, name="w2_scales", align_bytes=64)
        nc.vector.quantize_mx(
            out=w2_codes[:].bitcast(FP8X4), scales=w2_scales[:], in_=w2_bf[:].rearrange("p c j -> p (c j)")
        )
        for t in range(PACK + 1):
            if t < PACK:
                align(t, 0)
                align(t, 1)
            if t >= 1:
                distance(t - 1, 0)
                distance(t - 1, 1)
            if t + 1 < PACK:
                product(t + 1)
            if t < PACK:
                for step in (difference, gap_cost, magnitude):
                    step(t, 0)
                    step(t, 1)
            if t >= 1:
                kernel_value(t - 1, 0)
                kernel_value(t - 1, 1)
                scale_rows(t - 1)

        hid = keep.tile([P, PACK, U], F32, align_bytes=64, name="hid", tag="diff30")
        for t in range(PACK):
            width = CLONES if t < PACK - 1 else QUARTER
            for first in range(0, U, width):
                cols = slice(first, first + width)
                src = kern[t][:].indirect(entries(rep_t, first, first + width))
                if first >= CLONES and t != 2:
                    looked_up = keep.tile([P, width], F32, align_bytes=64, name="looked_up", tag=(("diff31", "mag31", "lu2", "lu3")[t]) if t < 3 else "lu3%d" % first)
                    nc.scalar.activation(looked_up[:], src, ACT.Copy)
                    src = looked_up[:]
                nc.vector.tensor_tensor(hid[:, t, cols], src, fr_t[:, t, cols], ALU.mult)

        hid_bf = {}
        for q in range(4):
            hid_bf[q] = keep.tile([P, QUARTER, PACK], BF16, name="hid_bf%d" % q, align_bytes=64)
            (nc.scalar.copy if q % 2 == 0 else nc.vector.tensor_copy)(
                hid_bf[q][:].rearrange("p (c i) t -> p c t i", i=4),
                hid[:, :, q * QUARTER : (q + 1) * QUARTER].rearrange("p t (c i) -> p c t i", i=4),
            )
        out_rows = out.rearrange("(b p) r -> p b r", p=P)
        for q in range(4):
            codes = keep.tile([P, QUARTER], U32, name="hid_codes%d" % q, align_bytes=64)
            scales = keep.tile([P, QUARTER], U8, name="hid_scales%d" % q, align_bytes=64)
            nc.vector.quantize_mx(out=codes[:].bitcast(FP8X4), scales=scales[:], in_=hid_bf[q][:].rearrange("p c t -> p (c t)"))
            bank = psum.tile([P, N // P, QUARTER], F32, name="out_bank", tag=("y0", "y1", "y2", "dist00")[q])
            for b in range(N // P):
                rows = slice(b * P, (b + 1) * P)
                nc.tensor.matmul_mx(
                    out=bank[:, b, :],
                    lhsT=w2_codes[:, rows].bitcast(FP8X4),
                    lhsT_scale=w2_scales[:, rows],
                    rhs=codes[:].bitcast(FP8X4),
                    rhs_scale=scales[:],
                    start=True,
                    stop=True,
                )
            result = keep.tile([P, N // P, QUARTER], F32, align_bytes=64, name="result%d" % q)
            if q == 3:
                nc.vector.tensor_copy(result[:], bank[:])
            else:
                nc.scalar.copy(result[:], bank[:])
            nc.sync.dma_start(out_rows[:, :, q * QUARTER : (q + 1) * QUARTER], result[:])
